import numpy as np
import ml_dtypes


def mxq(x, axis, fmt="e4m3"):
    dtype, down = {"e4m3": (ml_dtypes.float8_e4m3fn, 7), "e5m2": (ml_dtypes.float8_e5m2, 14)}[fmt]
    v = np.moveaxis(np.asarray(x, np.float32).astype(ml_dtypes.bfloat16).astype(np.float64), axis, -1)
    blocks = v.reshape(v.shape[:-1] + (-1, 32))
    amax = np.abs(blocks).max(-1, keepdims=True)
    byte = np.maximum(np.where(amax > 0, np.frexp(amax)[1] - 1 + 127, 0) - down, 1)
    scale = np.exp2(byte - 127.0)
    codes = (blocks / scale).astype(np.float32).astype(dtype).astype(np.float64)
    return np.moveaxis((codes * scale).reshape(v.shape), -1, axis)


WIDE = False


def mx_kscale(k):
    if not WIDE:
        return np.ones(k)
    levels = np.array([10, -10, 5, -5, 0])
    if k % 512:
        return np.exp2(np.random.permutation(np.resize(levels, k // 32))).repeat(32)
    a = np.empty((k // 512, 16))
    for p in range(k // 512):
        a[p, :8] = np.random.permutation(np.resize(levels, 8))
        for g in range(8):
            far = levels[np.abs(levels - a[p, g]) >= 10]
            a[p, g + 8] = far[np.random.randint(len(far))]
    return np.exp2(a.ravel()).repeat(32)


def f64(x):
    return np.asarray(x).astype(np.float64)


def striped(idx):
    return np.tile(idx.reshape(-1, 16).T, (8, 1)).astype(np.uint16)


def unstriped(offs):
    return offs[:16].T.reshape(-1).astype(np.int64)


E2M1 = np.array([0.0, 0.5, 1.0, 1.5, 2.0, 3.0, 4.0, 6.0, -0.0, -0.5, -1.0, -1.5, -2.0, -3.0, -4.0, -6.0])


def pack_weight(w, fmt):
    k, n = w.shape
    w = f64(np.asarray(w, np.float32).astype(ml_dtypes.bfloat16)).reshape(k // 32, 32, n)
    amax = np.abs(w).max(1)
    if fmt == "e4m3":
        byte = np.frexp(amax)[1] - 1 + 127 - 7
    else:
        mant, ex = np.frexp(amax / 6.0)
        byte = np.where(mant > 0.5, ex, ex - 1) + 127
    byte = np.clip(np.where(amax > 0, byte, 1), 1, 254)
    scaled = (w * np.exp2(127.0 - byte)[:, None, :]).reshape(k, n).astype(np.float32)
    by_word = np.ascontiguousarray(scaled.reshape(k // 512, 128, 4, n).transpose(0, 1, 3, 2))
    if fmt == "e4m3":
        words = by_word.astype(ml_dtypes.float8_e4m3fn).view(np.uint8)
    else:
        c = by_word.astype(ml_dtypes.float4_e2m1fn).view(np.uint8) & 0xF
        words = (c[..., 0::2] | (c[..., 1::2] << 4)).reshape(k // 512, 128, 2 * n)
    return np.ascontiguousarray(words), np.ascontiguousarray(byte.astype(np.uint8).reshape(k // 512, 16, n))


def unpack_weight(words, scales, fmt):
    g, _, n = scales.shape
    words = np.ascontiguousarray(words).reshape(g, 128, n, -1)
    if fmt == "e4m3":
        vals = words.view(ml_dtypes.float8_e4m3fn).astype(np.float64)
    else:
        nib = np.empty((g, 128, n, 4), np.uint8)
        nib[..., 0::2] = words & 0xF
        nib[..., 1::2] = words >> 4
        vals = E2M1[nib]
    vals = vals * np.repeat(np.exp2(scales.astype(np.float64) - 127.0), 8, axis=1)[..., None]
    return vals.transpose(0, 1, 3, 2).reshape(g * 512, n)


def relu2(v):
    return np.maximum(v, 0.0) ** 2


K, T, E, G, H, N = 1024, 512, 6, 2, 512, 256


def setup_inputs():
    n = np.random.standard_normal
    s = mx_kscale(K)
    u = mx_kscale(H)
    chosen = np.random.permutation(E)[:G]
    w1 = pack_weight(n((K, E * H)) / np.sqrt(K) / s[:, None] * np.tile(u, E), "e4m3")
    w2 = pack_weight(n((H, E * N)) / np.sqrt(H) / u[:, None] ** 2, "e4m3")
    return {
        "xT": (n((K, T)) * s[:, None]).astype(np.float32),
        "w1_words": w1[0],
        "w1_scales": w1[1],
        "w2_words": w2[0],
        "w2_scales": w2[1],
        "gate": np.stack([np.tile(r, (128, 1)) for r in np.random.uniform(0.2, 1.0, (G, T))]).astype(np.float32),
        "offs": striped((chosen[:, None] * H + np.arange(H)).reshape(-1)),
        "offs2": striped((chosen[:, None] * N + np.arange(N)).reshape(-1)),
    }


def reference(xT, w1_words, w1_scales, w2_words, w2_scales, gate, offs, offs2):
    idx, idx2 = unstriped(offs), unstriped(offs2)
    x = mxq(f64(xT), 0, "e4m3")
    w1 = unpack_weight(w1_words, w1_scales, "e4m3")[:, idx]
    w2 = unpack_weight(w2_words, w2_scales, "e4m3")[:, idx2]
    y = np.zeros((N, T))
    for r in range(G):
        h = f64(gate[r, :1]) * relu2(w1[:, r * H:(r + 1) * H].T @ x)
        y = y + w2[:, r * N:(r + 1) * N].T @ mxq(h, 0, "e4m3")
    return y

@@ -1,0 +1,253 @@
+from contextlib import ExitStack
+
+import concourse.mybir as mybir
+from concourse.masks import make_identity
+
+K, T, E, G, H, N = 1024, 512, 6, 2, 512, 256
+FLOPS = 2 * G * T * H * (K + N)
+
+F32 = mybir.dt.float32
+BF16 = mybir.dt.bfloat16
+I32 = mybir.dt.int32
+U32 = mybir.dt.uint32
+U16 = mybir.dt.uint16
+U8 = mybir.dt.uint8
+FP8X4 = mybir.dt.float8_e4m3fn_x4
+MULT = mybir.AluOpType.mult
+RELU = mybir.ActivationFunctionType.Relu
+COPY = mybir.ActivationFunctionType.Copy
+
+P = 128
+PACK = 4
+PASSES = K // (P * PACK)
+CHUNKS = T // P
+QUADS = 4
+CAST_ON_SCALAR = ((0, 0), (0, 1), (1, 0), (1, 1), (2, 0), (3, 0))
+X_LOADS = ((0, 1, 1), (1, 1, 1), (0, 2, 1), (1, 2, 1), (0, 3, 1), (1, 3, 1))
+
+
+def tile_moe_wsel_b_relu2_f_kernel(
+    tc, xT, w1_words, w1_scales, w2_words, w2_scales, gate, offs, offs2, out
+):
+    nc = tc.nc
+    with ExitStack() as ctx:
+        keep = ctx.enter_context(tc.tile_pool(name="keep", bufs=1))
+        ring = ctx.enter_context(tc.tile_pool(name="ring", bufs=3))
+        psum_z = ctx.enter_context(tc.psum_pool(name="psum_z", bufs=4))
+        psum_t = ctx.enter_context(tc.psum_pool(name="psum_t", bufs=2))
+        psum_o = ctx.enter_context(tc.psum_pool(name="psum_o", bufs=2))
+
+        list1 = keep.tile([P, G * H // 16], U16, name="list1")
+        list2 = keep.tile([P, G * N // 16], U16, name="list2")
+        w1_rows = keep.tile([P, E * H], U8, tag="rows", name="w1_rows", align_bytes=64)
+        w2_rows = keep.tile([P, E * N], U8, name="w2_rows", align_bytes=64)
+        w1_all = [keep.tile([P, E * H], U32, tag=f"words{s}", name=f"w1_all{s}", align_bytes=64) for s in range(PASSES)]
+        w1_sc = keep.tile([P, G * H], U8, name="w1_sc", align_bytes=64)
+        w2_sc = keep.tile([P, G * N], U8, name="w2_sc", align_bytes=64)
+        gate_rows = keep.tile([P, P], F32, name="gate_rows")
+        ident = keep.tile([P, P], F32, name="ident")
+
+        for first, last in ((32, 64), (64, P)):
+            nc.vector.memset(w1_rows[first:last, :].bitcast(I32), 0)
+        for first, last in ((0, 16), (32, 64), (64, P)):
+            nc.vector.memset(w2_rows[first:last, :].bitcast(I32), 0)
+        nc.gpsimd.memset(gate_rows[:], 0.0)
+        gate_flat = gate.rearrange("r a (c t) -> (r a c) t", t=P)
+        nc.gpsimd.dma_start(out=gate_rows[0 : G * CHUNKS, :], in_=gate_flat[0 : 129 * (G * CHUNKS - 1) + 1 : 129, :])
+        make_identity(nc, ident[:])
+        nc.gpsimd.memset(w1_sc[:].bitcast(I32), 0)
+        nc.gpsimd.memset(w2_sc[:].bitcast(I32), 0)
+
+        def load_x(piece, s, first, count):
+            rows = xT[s * P * PACK : (s + 1) * P * PACK, first * P : (first + count) * P]
+            nc.sync.dma_start(out=piece, in_=rows.rearrange("(p j) t -> p j t", j=PACK))
+            for c in range(count):
+                x_raw[first + c, s] = piece[:, :, c * P : (c + 1) * P]
+
+        x_raw = {}
+        nc.sync.dma_start(list1[:], offs)
+        for s in range(PASSES):
+            nc.sync.dma_start(
+                out=w1_rows[16 * s : 16 * (s + 1), :].bitcast(I32),
+                in_=w1_scales.bitcast(I32)[s].rearrange("(q j) c -> j q c", j=4),
+            )
+        nc.sync.dma_start(list2[:], offs2)
+        nc.sync.dma_start(out=w2_rows[16:32, :].bitcast(I32), in_=w2_scales.bitcast(I32)[0])
+        for s in range(PASSES):
+            nc.sync.dma_start(
+                out=w1_all[s][:].bitcast(I32),
+                in_=w1_words[s].rearrange("p n t -> p (n t)").bitcast(I32),
+            )
+        for s in range(PASSES):
+            x_first = keep.tile([P, PACK, P], F32, name=f"x_first{s}")
+            load_x(x_first[:], s, 0, 1)
+
+        gate_t = psum_t.tile([P, P], F32, tag="turn", name="gate_t")
+        nc.tensor.transpose(gate_t[:], gate_rows[:], ident[:])
+        gate_cols = keep.tile([P, G * CHUNKS], F32, name="gate_cols")
+        nc.scalar.activation(gate_cols[:], gate_t[:, 0 : G * CHUNKS], COPY)
+
+        w1_rows_sel = keep.tile([P, G * H], U8, name="w1_rows_sel", align_bytes=64)
+        nc.vector.tensor_copy(w1_rows_sel[:], w1_rows[:].indirect(list1[:]))
+        w2_rows_sel = keep.tile([P, G * N], U8, name="w2_rows_sel", align_bytes=64)
+        nc.vector.tensor_copy(w2_rows_sel[:], w2_rows[:].indirect(list2[:]))
+        for q in range(QUADS):
+            nc.sync.dma_start(
+                out=w1_sc[32 * q : 32 * q + 4 * PASSES, :].bitcast(I32),
+                in_=w1_rows_sel[q : 32 : 4, :].bitcast(I32),
+            )
+
+        x_rest = keep.tile([P, (CHUNKS - 1) * K], F32, tag="rows", name="x_rest", align_bytes=64)
+        at = 0
+        for s, first, count in X_LOADS:
+            width = PACK * P * count
+            load_x(x_rest[:, at : at + width].rearrange("p (j t) -> p j t", j=PACK), s, first, count)
+            at = at + width
+        for q in range(QUADS):
+            nc.sync.dma_start(
+                out=w2_sc[32 * q : 32 * q + 4, :].bitcast(I32),
+                in_=w2_rows_sel[16 + 4 * q : 20 + 4 * q, :].bitcast(I32),
+            )
+
+        w1_first = keep.tile([P, G * H], U32, name="w1_first", align_bytes=64)
+        nc.vector.tensor_copy(w1_first[:], w1_all[0][:].indirect(list1[:]))
+        w2_all = keep.tile([P, E * N], U32, tag="words0", name="w2_all", align_bytes=64)
+        nc.sync.dma_start(
+            out=w2_all[:].bitcast(I32),
+            in_=w2_words[0].rearrange("p n t -> p (n t)").bitcast(I32),
+        )
+        w1_sel = {}
+        for r in range(G):
+            w1_sel[0, r] = w1_first[:, r * H : (r + 1) * H]
+            second = keep.tile([P, H], U32, name=f"w1_second{r}", align_bytes=64)
+            nc.vector.tensor_copy(second[:], w1_all[1][:].indirect(list1[:, r * H // 16 : (r + 1) * H // 16]))
+            w1_sel[1, r] = second[:]
+        w2_sel = keep.tile([P, G * N], U32, name="w2_sel", align_bytes=64)
+
+        x_codes, x_scales, x_grouped, z, turned, h_codes, h_scales = {}, {}, {}, {}, {}, {}, {}
+
+        def cast_x(c, s):
+            grouped = keep.tile([P, P, PACK], BF16, name=f"x_grouped{c}_{s}", align_bytes=64)
+            dst = grouped[:].rearrange("p (b i) j -> p b j i", i=4)
+            src = x_raw[c, s].rearrange("p j (b i) -> p b j i", i=4)
+            if (c, s) in CAST_ON_SCALAR:
+                nc.scalar.copy(dst, src)
+            else:
+                nc.vector.tensor_copy(dst, src)
+            x_grouped[c, s] = grouped
+
+        def quantize_x(c, s):
+            x_codes[c, s] = keep.tile([P, P], U32, name=f"x_codes{c}_{s}", align_bytes=64)
+            x_scales[c, s] = keep.tile([P, P], U8, name=f"x_scales{c}_{s}", align_bytes=64)
+            nc.vector.quantize_mx(
+                out=x_codes[c, s][:].bitcast(FP8X4),
+                scales=x_scales[c, s][:],
+                in_=x_grouped[c, s][:].rearrange("p t j -> p (t j)"),
+            )
+
+        def first_product(c):
+            for r in range(G):
+                z[c, r] = psum_z.tile([P, H], F32, tag="z", name=f"z{c}_{r}")
+                for s in range(PASSES):
+                    nc.tensor.matmul_mx(
+                        out=z[c, r][:],
+                        lhsT=x_codes[c, s][:].bitcast(FP8X4),
+                        lhsT_scale=x_scales[c, s][:],
+                        rhs=w1_sel[s, r].bitcast(FP8X4),
+                        rhs_scale=w1_sc[4 * s : P, r * H : (r + 1) * H],
+                        start=(s == 0),
+                        stop=(s == PASSES - 1),
+                    )
+
+        def hidden(c):
+            if c < CHUNKS - 1:
+                both = psum_t.tile([P, G, 2, P], F32, tag="turn", name=f"turned{c}")
+            for r in range(G):
+                relu = ring.tile([P, H], F32, tag="relu", name=f"relu{c}_{r}")
+                nc.scalar.activation(
+                    relu[:].rearrange("p (u q e) -> p u q e", u=2, e=2),
+                    z[c, r][:].rearrange("p (q u e) -> p u q e", u=2, e=2),
+                    RELU,
+                )
+                h = ring.tile([P, H], BF16, tag="h", name=f"h{c}_{r}", align_bytes=64)
+                col = r * CHUNKS + c
+                nc.vector.scalar_tensor_tensor(h[:], relu[:], gate_cols[:, col : col + 1], relu[:], MULT, MULT)
+                if c < CHUNKS - 1:
+                    turned[c, r] = both[:, r : r + 1]
+                    turned[c] = both[:]
+                else:
+                    alone = psum_z.tile([P, 1, 2, P], F32, tag="z", name=f"turned{c}_{r}")
+                    turned[c, r] = alone[:]
+                pairs = h[:].bitcast(F32)
+                for u in range(2):
+                    nc.tensor.transpose(turned[c, r][:, 0, u, :], pairs[:, u * P : (u + 1) * P], ident[:])
+
+        def quantize_h(c, source, experts):
+            width = len(experts) * P
+            name = f"{c}_{experts[0]}"
+            grouped = ring.tile([P, width * PACK], BF16, tag="h_grouped", name="h_grouped" + name, align_bytes=64)
+            nc.scalar.copy(
+                grouped[:].bitcast(F32).rearrange("p (r t u) -> p r t u", t=P, u=2),
+                source.rearrange("p r u t -> p r t u"),
+            )
+            codes = keep.tile([P, width], U32, name="h_codes" + name, align_bytes=64)
+            scales = keep.tile([P, width], U8, name="h_scales" + name, align_bytes=64)
+            nc.vector.quantize_mx(out=codes[:].bitcast(FP8X4), scales=scales[:], in_=grouped[:])
+            for at, r in enumerate(experts):
+                h_codes[c, r] = codes[:, at * P : (at + 1) * P]
+                h_scales[c, r] = scales[:, at * P : (at + 1) * P]
+
+        def second_pass(target, c, a, r):
+            cols = slice(r * N + a * P, r * N + (a + 1) * P)
+            nc.tensor.matmul_mx(
+                out=target,
+                lhsT=w2_sel[:, cols].bitcast(FP8X4),
+                lhsT_scale=w2_sc[:, cols],
+                rhs=h_codes[c, r].bitcast(FP8X4),
+                rhs_scale=h_scales[c, r],
+                start=(r == 0),
+                stop=(r == G - 1),
+            )
+
+        out_view = out.rearrange("(a p) t -> p a t", p=P)
+
+        def second_product(c):
+            acc = psum_o.tile([P, N // P, P], F32, tag="acc", name=f"acc{c}")
+            for a in range(N // P):
+                for r in range(G):
+                    second_pass(acc[:, a, :], c, a, r)
+            result = ring.tile([P, N // P, P], F32, tag="result", name=f"result{c}")
+            nc.scalar.copy(result[:], acc[:])
+            nc.sync.dma_start(out=out_view[:, :, c * P : (c + 1) * P], in_=result[:])
+
+        def last_second_product(c):
+            accs = [psum_z.tile([P, P], F32, tag="z", name=f"last_acc{a}") for a in range(N // P)]
+            for r in range(G):
+                for a in range(N // P):
+                    second_pass(accs[a][:], c, a, r)
+            result = ring.tile([P, N // P, P], F32, tag="result", name=f"result{c}")
+            nc.scalar.copy(result[:, 0, :], accs[0][:])
+            nc.vector.tensor_copy(result[:, 1, :], accs[1][:])
+            nc.sync.dma_start(out=out_view[:, :, c * P : (c + 1) * P], in_=result[:])
+
+        last = CHUNKS - 1
+        for step in range(CHUNKS + 3):
+            if step < CHUNKS:
+                for s in range(PASSES):
+                    cast_x(step, s)
+                for s in range(PASSES):
+                    quantize_x(step, s)
+                first_product(step)
+            if 0 <= step - 1 < CHUNKS:
+                hidden(step - 1)
+            if step == 3:
+                nc.vector.tensor_copy(w2_sel[:], w2_all[:].indirect(list2[:]))
+            if 0 <= step - 2 < last:
+                quantize_h(step - 2, turned[step - 2], (0, 1))
+            if step - 2 == last:
+                for r in range(G):
+                    quantize_h(last, turned[last, r], (r,))
+            if 0 <= step - 3 < last:
+                second_product(step - 3)
+            if step - 3 == last:
+                last_second_product(last)

@@ -21,9 +21,18 @@ P = 128
 PACK = 4
 PASSES = K // (P * PACK)
 CHUNKS = T // P
-QUADS = 4
-CAST_ON_SCALAR = ((0, 0), (0, 1), (1, 0), (1, 1), (2, 0), (3, 0))
-X_LOADS = ((0, 1, 1), (1, 1, 1), (0, 2, 1), (1, 2, 1), (0, 3, 1), (1, 3, 1))
+LAST = CHUNKS - 1
+OUT_TILES = N // P
+QUAD = 32
+QUADS = P // QUAD
+QUAD_BLOCKS = 4
+PASS_BLOCKS = QUADS * QUAD_BLOCKS
+LIST_GROUP = 16
+GATE_ROWS = G * CHUNKS
+
+VECTOR_CAST_CHUNK = 2
+W2_GATHER_STEP = 2
+SUM_BANKS, TURN_BANKS, RESULT_BANKS = 4, 2, 2
 
 
 def tile_moe_wsel_b_relu2_f_kernel(
@@ -32,60 +41,67 @@ def tile_moe_wsel_b_relu2_f_kernel(
     nc = tc.nc
     with ExitStack() as ctx:
         keep = ctx.enter_context(tc.tile_pool(name="keep", bufs=1))
-        ring = ctx.enter_context(tc.tile_pool(name="ring", bufs=3))
-        psum_z = ctx.enter_context(tc.psum_pool(name="psum_z", bufs=4))
-        psum_t = ctx.enter_context(tc.psum_pool(name="psum_t", bufs=2))
-        psum_o = ctx.enter_context(tc.psum_pool(name="psum_o", bufs=2))
+        stage = ctx.enter_context(tc.tile_pool(name="stage", bufs=G * CHUNKS))
+        psum_sum = ctx.enter_context(tc.psum_pool(name="psum_sum", bufs=SUM_BANKS))
+        psum_turn = ctx.enter_context(tc.psum_pool(name="psum_turn", bufs=TURN_BANKS))
+        psum_result = ctx.enter_context(tc.psum_pool(name="psum_result", bufs=RESULT_BANKS))
 
-        list1 = keep.tile([P, G * H // 16], U16, name="list1")
-        list2 = keep.tile([P, G * N // 16], U16, name="list2")
-        w1_rows = keep.tile([P, E * H], U8, tag="rows", name="w1_rows", align_bytes=64)
+        list1 = keep.tile([P, G * H // LIST_GROUP], U16, name="list1")
+        list2 = keep.tile([P, G * N // LIST_GROUP], U16, name="list2")
+        w1_rows = keep.tile([P, E * H], U8, tag="rows_then_x", name="w1_rows", align_bytes=64)
         w2_rows = keep.tile([P, E * N], U8, name="w2_rows", align_bytes=64)
         w1_all = [keep.tile([P, E * H], U32, tag=f"words{s}", name=f"w1_all{s}", align_bytes=64) for s in range(PASSES)]
-        w1_sc = keep.tile([P, G * H], U8, name="w1_sc", align_bytes=64)
-        w2_sc = keep.tile([P, G * N], U8, name="w2_sc", align_bytes=64)
+        w1_planes = keep.tile([P, G * H], U8, name="w1_planes", align_bytes=64)
+        w2_plane = keep.tile([P, G * N], U8, name="w2_plane", align_bytes=64)
         gate_rows = keep.tile([P, P], F32, name="gate_rows")
         ident = keep.tile([P, P], F32, name="ident")
 
-        for first, last in ((32, 64), (64, P)):
-            nc.vector.memset(w1_rows[first:last, :].bitcast(I32), 0)
-        for first, last in ((0, 16), (32, 64), (64, P)):
-            nc.vector.memset(w2_rows[first:last, :].bitcast(I32), 0)
-        nc.gpsimd.memset(gate_rows[:], 0.0)
-        gate_flat = gate.rearrange("r a (c t) -> (r a c) t", t=P)
-        nc.gpsimd.dma_start(out=gate_rows[0 : G * CHUNKS, :], in_=gate_flat[0 : 129 * (G * CHUNKS - 1) + 1 : 129, :])
+        w2_from = QUAD - PASS_BLOCKS
+        gate_from = QUAD - GATE_ROWS
+        upper = ((QUAD, 2 * QUAD), (2 * QUAD, P))
+        for lo, hi in upper:
+            nc.vector.memset(w1_rows[lo:hi, :].bitcast(I32), 0)
+        for lo, hi in ((0, w2_from),) + upper:
+            nc.vector.memset(w2_rows[lo:hi, :].bitcast(I32), 0)
+        for lo, hi in ((0, gate_from),) + upper:
+            nc.gpsimd.memset(gate_rows[lo:hi, :], 0.0)
         make_identity(nc, ident[:])
-        nc.gpsimd.memset(w1_sc[:].bitcast(I32), 0)
-        nc.gpsimd.memset(w2_sc[:].bitcast(I32), 0)
-
-        def load_x(piece, s, first, count):
-            rows = xT[s * P * PACK : (s + 1) * P * PACK, first * P : (first + count) * P]
-            nc.sync.dma_start(out=piece, in_=rows.rearrange("(p j) t -> p j t", j=PACK))
-            for c in range(count):
-                x_raw[first + c, s] = piece[:, :, c * P : (c + 1) * P]
+        nc.gpsimd.memset(w1_planes[:].bitcast(I32), 0)
+        nc.gpsimd.memset(w2_plane[:].bitcast(I32), 0)
 
         x_raw = {}
+
+        def load_x(piece, c, s):
+            rows = xT[s * P * PACK : (s + 1) * P * PACK, c * P : (c + 1) * P]
+            nc.sync.dma_start(out=piece, in_=rows.rearrange("(p d) t -> p d t", d=PACK))
+            x_raw[c, s] = piece
+
+        def load_words(tile, words):
+            nc.sync.dma_start(out=tile[:].bitcast(I32), in_=words.rearrange("p n d -> p (n d)").bitcast(I32))
+
         nc.sync.dma_start(list1[:], offs)
         for s in range(PASSES):
             nc.sync.dma_start(
-                out=w1_rows[16 * s : 16 * (s + 1), :].bitcast(I32),
-                in_=w1_scales.bitcast(I32)[s].rearrange("(q j) c -> j q c", j=4),
+                out=w1_rows[PASS_BLOCKS * s : PASS_BLOCKS * (s + 1), :].bitcast(I32),
+                in_=w1_scales.bitcast(I32)[s].rearrange("(q j) m -> j q m", j=QUAD_BLOCKS),
             )
         nc.sync.dma_start(list2[:], offs2)
-        nc.sync.dma_start(out=w2_rows[16:32, :].bitcast(I32), in_=w2_scales.bitcast(I32)[0])
+        nc.sync.dma_start(out=w2_rows[w2_from:QUAD, :].bitcast(I32), in_=w2_scales.bitcast(I32)[0])
+        gate_pieces = gate.rearrange("r a (c t) -> (r a c) t", t=P)
+        gate_step = P + 1
+        nc.sync.dma_start(
+            out=gate_rows[gate_from:QUAD, :], in_=gate_pieces[0 : gate_step * (GATE_ROWS - 1) + 1 : gate_step, :]
+        )
         for s in range(PASSES):
-            nc.sync.dma_start(
-                out=w1_all[s][:].bitcast(I32),
-                in_=w1_words[s].rearrange("p n t -> p (n t)").bitcast(I32),
-            )
+            load_words(w1_all[s], w1_words[s])
         for s in range(PASSES):
             x_first = keep.tile([P, PACK, P], F32, name=f"x_first{s}")
-            load_x(x_first[:], s, 0, 1)
+            load_x(x_first[:], 0, s)
 
-        gate_t = psum_t.tile([P, P], F32, tag="turn", name="gate_t")
-        nc.tensor.transpose(gate_t[:], gate_rows[:], ident[:])
-        gate_cols = keep.tile([P, G * CHUNKS], F32, name="gate_cols")
-        nc.scalar.activation(gate_cols[:], gate_t[:, 0 : G * CHUNKS], COPY)
+        gate_turned = psum_turn.tile([P, P], F32, tag="turn", name="gate_turned")
+        nc.tensor.transpose(gate_turned[:], gate_rows[:], ident[:])
+        gate_cols = keep.tile([P, GATE_ROWS], F32, name="gate_cols")
+        nc.scalar.activation(gate_cols[:], gate_turned[:, gate_from:QUAD], COPY)
 
         w1_rows_sel = keep.tile([P, G * H], U8, name="w1_rows_sel", align_bytes=64)
         nc.vector.tensor_copy(w1_rows_sel[:], w1_rows[:].indirect(list1[:]))
@@ -93,47 +109,47 @@ def tile_moe_wsel_b_relu2_f_kernel(
         nc.vector.tensor_copy(w2_rows_sel[:], w2_rows[:].indirect(list2[:]))
         for q in range(QUADS):
             nc.sync.dma_start(
-                out=w1_sc[32 * q : 32 * q + 4 * PASSES, :].bitcast(I32),
-                in_=w1_rows_sel[q : 32 : 4, :].bitcast(I32),
+                out=w1_planes[QUAD * q : QUAD * q + QUAD_BLOCKS * PASSES, :].bitcast(I32),
+                in_=w1_rows_sel[q:QUAD:QUADS, :].bitcast(I32),
             )
 
-        x_rest = keep.tile([P, (CHUNKS - 1) * K], F32, tag="rows", name="x_rest", align_bytes=64)
-        at = 0
-        for s, first, count in X_LOADS:
-            width = PACK * P * count
-            load_x(x_rest[:, at : at + width].rearrange("p (j t) -> p j t", j=PACK), s, first, count)
-            at = at + width
+        w1_sel_first = keep.tile([P, G * H], U32, name="w1_sel_first", align_bytes=64)
+        nc.vector.tensor_copy(w1_sel_first[:], w1_all[0][:].indirect(list1[:]))
+
+        x_rest = keep.tile([P, LAST * K], F32, tag="rows_then_x", name="x_rest", align_bytes=64)
+        for c in range(1, CHUNKS):
+            if c == LAST:
+                w2_all = keep.tile([P, E * N], U32, tag="words0", name="w2_all", align_bytes=64)
+                load_words(w2_all, w2_words[0])
+            for s in range(PASSES):
+                at = ((c - 1) * PASSES + s) * PACK * P
+                load_x(x_rest[:, at : at + PACK * P].rearrange("p (d t) -> p d t", d=PACK), c, s)
         for q in range(QUADS):
+            row = w2_from + QUAD_BLOCKS * q
             nc.sync.dma_start(
-                out=w2_sc[32 * q : 32 * q + 4, :].bitcast(I32),
-                in_=w2_rows_sel[16 + 4 * q : 20 + 4 * q, :].bitcast(I32),
+                out=w2_plane[QUAD * q : QUAD * q + QUAD_BLOCKS, :].bitcast(I32),
+                in_=w2_rows_sel[row : row + QUAD_BLOCKS, :].bitcast(I32),
             )
 
-        w1_first = keep.tile([P, G * H], U32, name="w1_first", align_bytes=64)
-        nc.vector.tensor_copy(w1_first[:], w1_all[0][:].indirect(list1[:]))
-        w2_all = keep.tile([P, E * N], U32, tag="words0", name="w2_all", align_bytes=64)
-        nc.sync.dma_start(
-            out=w2_all[:].bitcast(I32),
-            in_=w2_words[0].rearrange("p n t -> p (n t)").bitcast(I32),
-        )
         w1_sel = {}
         for r in range(G):
-            w1_sel[0, r] = w1_first[:, r * H : (r + 1) * H]
-            second = keep.tile([P, H], U32, name=f"w1_second{r}", align_bytes=64)
-            nc.vector.tensor_copy(second[:], w1_all[1][:].indirect(list1[:, r * H // 16 : (r + 1) * H // 16]))
+            w1_sel[0, r] = w1_sel_first[:, r * H : (r + 1) * H]
+            second = keep.tile([P, H], U32, name=f"w1_sel_second{r}", align_bytes=64)
+            entries = list1[:, r * H // LIST_GROUP : (r + 1) * H // LIST_GROUP]
+            nc.vector.tensor_copy(second[:], w1_all[1][:].indirect(entries))
             w1_sel[1, r] = second[:]
         w2_sel = keep.tile([P, G * N], U32, name="w2_sel", align_bytes=64)
 
-        x_codes, x_scales, x_grouped, z, turned, h_codes, h_scales = {}, {}, {}, {}, {}, {}, {}
+        x_grouped, x_codes, x_scales, sums, turned, h_codes, h_scales = {}, {}, {}, {}, {}, {}, {}
 
         def cast_x(c, s):
             grouped = keep.tile([P, P, PACK], BF16, name=f"x_grouped{c}_{s}", align_bytes=64)
-            dst = grouped[:].rearrange("p (b i) j -> p b j i", i=4)
-            src = x_raw[c, s].rearrange("p j (b i) -> p b j i", i=4)
-            if (c, s) in CAST_ON_SCALAR:
-                nc.scalar.copy(dst, src)
-            else:
+            dst = grouped[:].rearrange("p (b e) d -> p b d e", e=4)
+            src = x_raw[c, s].rearrange("p d (b e) -> p b d e", e=4)
+            if c == VECTOR_CAST_CHUNK:
                 nc.vector.tensor_copy(dst, src)
+            else:
+                nc.scalar.copy(dst, src)
             x_grouped[c, s] = grouped
 
         def quantize_x(c, s):
@@ -142,41 +158,41 @@ def tile_moe_wsel_b_relu2_f_kernel(
             nc.vector.quantize_mx(
                 out=x_codes[c, s][:].bitcast(FP8X4),
                 scales=x_scales[c, s][:],
-                in_=x_grouped[c, s][:].rearrange("p t j -> p (t j)"),
+                in_=x_grouped[c, s][:].rearrange("p t d -> p (t d)"),
             )
 
         def first_product(c):
             for r in range(G):
-                z[c, r] = psum_z.tile([P, H], F32, tag="z", name=f"z{c}_{r}")
+                sums[c, r] = psum_sum.tile([P, H], F32, tag="sum", name=f"sums{c}_{r}")
                 for s in range(PASSES):
                     nc.tensor.matmul_mx(
-                        out=z[c, r][:],
+                        out=sums[c, r][:],
                         lhsT=x_codes[c, s][:].bitcast(FP8X4),
                         lhsT_scale=x_scales[c, s][:],
                         rhs=w1_sel[s, r].bitcast(FP8X4),
-                        rhs_scale=w1_sc[4 * s : P, r * H : (r + 1) * H],
+                        rhs_scale=w1_planes[QUAD_BLOCKS * s : P, r * H : (r + 1) * H],
                         start=(s == 0),
                         stop=(s == PASSES - 1),
                     )
 
         def hidden(c):
-            if c < CHUNKS - 1:
-                both = psum_t.tile([P, G, 2, P], F32, tag="turn", name=f"turned{c}")
+            if c < LAST:
+                both = psum_turn.tile([P, G, 2, P], F32, tag="turn", name=f"turned{c}")
+                turned[c] = both[:]
             for r in range(G):
-                relu = ring.tile([P, H], F32, tag="relu", name=f"relu{c}_{r}")
+                relu = stage.tile([P, H], F32, tag="relu", name=f"relu{c}_{r}")
                 nc.scalar.activation(
-                    relu[:].rearrange("p (u q e) -> p u q e", u=2, e=2),
-                    z[c, r][:].rearrange("p (q u e) -> p u q e", u=2, e=2),
+                    relu[:].rearrange("t (u p e) -> t u p e", u=2, e=2),
+                    sums[c, r][:].rearrange("t (p u e) -> t u p e", u=2, e=2),
                     RELU,
                 )
-                h = ring.tile([P, H], BF16, tag="h", name=f"h{c}_{r}", align_bytes=64)
+                h = stage.tile([P, H], BF16, tag="h", name=f"h{c}_{r}", align_bytes=64)
                 col = r * CHUNKS + c
                 nc.vector.scalar_tensor_tensor(h[:], relu[:], gate_cols[:, col : col + 1], relu[:], MULT, MULT)
-                if c < CHUNKS - 1:
+                if c < LAST:
                     turned[c, r] = both[:, r : r + 1]
-                    turned[c] = both[:]
                 else:
-                    alone = psum_z.tile([P, 1, 2, P], F32, tag="z", name=f"turned{c}_{r}")
+                    alone = psum_sum.tile([P, 1, 2, P], F32, tag="sum", name=f"turned{c}_{r}")
                     turned[c, r] = alone[:]
                 pairs = h[:].bitcast(F32)
                 for u in range(2):
@@ -184,25 +200,25 @@ def tile_moe_wsel_b_relu2_f_kernel(
 
         def quantize_h(c, source, experts):
             width = len(experts) * P
-            name = f"{c}_{experts[0]}"
-            grouped = ring.tile([P, width * PACK], BF16, tag="h_grouped", name="h_grouped" + name, align_bytes=64)
+            label = f"{c}_{experts[0]}"
+            grouped = stage.tile([P, width * PACK], BF16, tag="h_grouped", name="h_grouped" + label, align_bytes=64)
             nc.scalar.copy(
                 grouped[:].bitcast(F32).rearrange("p (r t u) -> p r t u", t=P, u=2),
                 source.rearrange("p r u t -> p r t u"),
             )
-            codes = keep.tile([P, width], U32, name="h_codes" + name, align_bytes=64)
-            scales = keep.tile([P, width], U8, name="h_scales" + name, align_bytes=64)
+            codes = keep.tile([P, width], U32, name="h_codes" + label, align_bytes=64)
+            scales = keep.tile([P, width], U8, name="h_scales" + label, align_bytes=64)
             nc.vector.quantize_mx(out=codes[:].bitcast(FP8X4), scales=scales[:], in_=grouped[:])
-            for at, r in enumerate(experts):
-                h_codes[c, r] = codes[:, at * P : (at + 1) * P]
-                h_scales[c, r] = scales[:, at * P : (at + 1) * P]
+            for place, r in enumerate(experts):
+                h_codes[c, r] = codes[:, place * P : (place + 1) * P]
+                h_scales[c, r] = scales[:, place * P : (place + 1) * P]
 
         def second_pass(target, c, a, r):
             cols = slice(r * N + a * P, r * N + (a + 1) * P)
             nc.tensor.matmul_mx(
                 out=target,
                 lhsT=w2_sel[:, cols].bitcast(FP8X4),
-                lhsT_scale=w2_sc[:, cols],
+                lhsT_scale=w2_plane[:, cols],
                 rhs=h_codes[c, r].bitcast(FP8X4),
                 rhs_scale=h_scales[c, r],
                 start=(r == 0),
@@ -212,26 +228,25 @@ def tile_moe_wsel_b_relu2_f_kernel(
         out_view = out.rearrange("(a p) t -> p a t", p=P)
 
         def second_product(c):
-            acc = psum_o.tile([P, N // P, P], F32, tag="acc", name=f"acc{c}")
-            for a in range(N // P):
+            acc = psum_result.tile([P, OUT_TILES, P], F32, tag="acc", name=f"acc{c}")
+            for a in range(OUT_TILES):
                 for r in range(G):
                     second_pass(acc[:, a, :], c, a, r)
-            result = ring.tile([P, N // P, P], F32, tag="result", name=f"result{c}")
+            result = stage.tile([P, OUT_TILES, P], F32, tag="result", name=f"result{c}")
             nc.scalar.copy(result[:], acc[:])
             nc.sync.dma_start(out=out_view[:, :, c * P : (c + 1) * P], in_=result[:])
 
         def last_second_product(c):
-            accs = [psum_z.tile([P, P], F32, tag="z", name=f"last_acc{a}") for a in range(N // P)]
+            accs = [psum_sum.tile([P, P], F32, tag="sum", name=f"last_acc{a}") for a in range(OUT_TILES)]
             for r in range(G):
-                for a in range(N // P):
+                for a in range(OUT_TILES):
                     second_pass(accs[a][:], c, a, r)
-            result = ring.tile([P, N // P, P], F32, tag="result", name=f"result{c}")
+            result = stage.tile([P, OUT_TILES, P], F32, tag="result", name=f"result{c}")
             nc.scalar.copy(result[:, 0, :], accs[0][:])
             nc.vector.tensor_copy(result[:, 1, :], accs[1][:])
             nc.sync.dma_start(out=out_view[:, :, c * P : (c + 1) * P], in_=result[:])
 
-        last = CHUNKS - 1
-        for step in range(CHUNKS + 3):
+        for step in range(CHUNKS + 2):
             if step < CHUNKS:
                 for s in range(PASSES):
                     cast_x(step, s)
@@ -240,14 +255,12 @@ def tile_moe_wsel_b_relu2_f_kernel(
                 first_product(step)
             if 0 <= step - 1 < CHUNKS:
                 hidden(step - 1)
-            if step == 3:
+            if step == W2_GATHER_STEP:
                 nc.vector.tensor_copy(w2_sel[:], w2_all[:].indirect(list2[:]))
-            if 0 <= step - 2 < last:
-                quantize_h(step - 2, turned[step - 2], (0, 1))
-            if step - 2 == last:
+            if 0 <= step - 2 < LAST:
+                quantize_h(step - 2, turned[step - 2], tuple(range(G)))
+                second_product(step - 2)
+            if step - 2 == LAST:
                 for r in range(G):
-                    quantize_h(last, turned[last, r], (r,))
-            if 0 <= step - 3 < last:
-                second_product(step - 3)
-            if step - 3 == last:
-                last_second_product(last)
+                    quantize_h(LAST, turned[LAST, r], (r,))
+                last_second_product(LAST)

@@ -33,6 +33,7 @@ GATE_ROWS = G * CHUNKS
 VECTOR_CAST_CHUNK = 2
 W2_GATHER_STEP = 2
 SUM_BANKS, TURN_BANKS, RESULT_BANKS = 4, 2, 2
+WARM_PASSES = 5
 
 
 def tile_moe_wsel_b_relu2_f_kernel(
@@ -115,6 +116,17 @@ def tile_moe_wsel_b_relu2_f_kernel(
 
         w1_sel_first = keep.tile([P, G * H], U32, name="w1_sel_first", align_bytes=64)
         nc.vector.tensor_copy(w1_sel_first[:], w1_all[0][:].indirect(list1[:]))
+        warm = psum_result.tile([P, H], F32, tag="acc", name="warm")
+        for k in range(WARM_PASSES):
+            nc.tensor.matmul_mx(
+                out=warm[:],
+                lhsT=w1_sel_first[:, 0:P].bitcast(FP8X4),
+                lhsT_scale=w1_rows_sel[:, 0:P],
+                rhs=w1_sel_first[:, 0:H].bitcast(FP8X4),
+                rhs_scale=w1_rows_sel[:, 0:H],
+                start=True,
+                stop=True,
+            )
 
         x_rest = keep.tile([P, LAST * K], F32, tag="rows_then_x", name="x_rest", align_bytes=64)
         for c in range(1, CHUNKS):

@@ -33,7 +33,7 @@ GATE_ROWS = G * CHUNKS
 VECTOR_CAST_CHUNK = 2
 W2_GATHER_STEP = 2
 SUM_BANKS, TURN_BANKS, RESULT_BANKS = 4, 2, 2
-WARM_PASSES = 5
+WARM_PASSES = 4
 
 
 def tile_moe_wsel_b_relu2_f_kernel(
@@ -57,15 +57,12 @@ def tile_moe_wsel_b_relu2_f_kernel(
         gate_rows = keep.tile([P, P], F32, name="gate_rows")
         ident = keep.tile([P, P], F32, name="ident")
 
-        w2_from = QUAD - PASS_BLOCKS
-        gate_from = QUAD - GATE_ROWS
-        upper = ((QUAD, 2 * QUAD), (2 * QUAD, P))
-        for lo, hi in upper:
-            nc.vector.memset(w1_rows[lo:hi, :].bitcast(I32), 0)
-        for lo, hi in ((0, w2_from),) + upper:
-            nc.vector.memset(w2_rows[lo:hi, :].bitcast(I32), 0)
-        for lo, hi in ((0, gate_from),) + upper:
-            nc.gpsimd.memset(gate_rows[lo:hi, :], 0.0)
+        w1_from = P - PASSES * PASS_BLOCKS
+        w2_from = P - PASS_BLOCKS
+        gate_from = P - GATE_ROWS
+        nc.vector.memset(w1_rows[0:w1_from, :].bitcast(I32), 0)
+        nc.vector.memset(w2_rows[0:w2_from, :].bitcast(I32), 0)
+        nc.gpsimd.memset(gate_rows[0:gate_from, :], 0.0)
         make_identity(nc, ident[:])
         nc.gpsimd.memset(w1_planes[:].bitcast(I32), 0)
         nc.gpsimd.memset(w2_plane[:].bitcast(I32), 0)
@@ -83,15 +80,15 @@ def tile_moe_wsel_b_relu2_f_kernel(
         nc.sync.dma_start(list1[:], offs)
         for s in range(PASSES):
             nc.sync.dma_start(
-                out=w1_rows[PASS_BLOCKS * s : PASS_BLOCKS * (s + 1), :].bitcast(I32),
+                out=w1_rows[w1_from + PASS_BLOCKS * s : w1_from + PASS_BLOCKS * (s + 1), :].bitcast(I32),
                 in_=w1_scales.bitcast(I32)[s].rearrange("(q j) m -> j q m", j=QUAD_BLOCKS),
             )
         nc.sync.dma_start(list2[:], offs2)
-        nc.sync.dma_start(out=w2_rows[w2_from:QUAD, :].bitcast(I32), in_=w2_scales.bitcast(I32)[0])
+        nc.sync.dma_start(out=w2_rows[w2_from:P, :].bitcast(I32), in_=w2_scales.bitcast(I32)[0])
         gate_pieces = gate.rearrange("r a (c t) -> (r a c) t", t=P)
         gate_step = P + 1
         nc.sync.dma_start(
-            out=gate_rows[gate_from:QUAD, :], in_=gate_pieces[0 : gate_step * (GATE_ROWS - 1) + 1 : gate_step, :]
+            out=gate_rows[gate_from:P, :], in_=gate_pieces[0 : gate_step * (GATE_ROWS - 1) + 1 : gate_step, :]
         )
         for s in range(PASSES):
             load_words(w1_all[s], w1_words[s])
@@ -102,7 +99,7 @@ def tile_moe_wsel_b_relu2_f_kernel(
         gate_turned = psum_turn.tile([P, P], F32, tag="turn", name="gate_turned")
         nc.tensor.transpose(gate_turned[:], gate_rows[:], ident[:])
         gate_cols = keep.tile([P, GATE_ROWS], F32, name="gate_cols")
-        nc.scalar.activation(gate_cols[:], gate_turned[:, gate_from:QUAD], COPY)
+        nc.scalar.activation(gate_cols[:], gate_turned[:, gate_from:P], COPY)
 
         w1_rows_sel = keep.tile([P, G * H], U8, name="w1_rows_sel", align_bytes=64)
         nc.vector.tensor_copy(w1_rows_sel[:], w1_rows[:].indirect(list1[:]))
@@ -111,7 +108,7 @@ def tile_moe_wsel_b_relu2_f_kernel(
         for q in range(QUADS):
             nc.sync.dma_start(
                 out=w1_planes[QUAD * q : QUAD * q + QUAD_BLOCKS * PASSES, :].bitcast(I32),
-                in_=w1_rows_sel[q:QUAD:QUADS, :].bitcast(I32),
+                in_=w1_rows_sel[w1_from + q : P : QUADS, :].bitcast(I32),
             )
 
         w1_sel_first = keep.tile([P, G * H], U32, name="w1_sel_first", align_bytes=64)
@@ -130,12 +127,11 @@ def tile_moe_wsel_b_relu2_f_kernel(
 
         x_rest = keep.tile([P, LAST * K], F32, tag="rows_then_x", name="x_rest", align_bytes=64)
         for c in range(1, CHUNKS):
-            if c == LAST:
-                w2_all = keep.tile([P, E * N], U32, tag="words0", name="w2_all", align_bytes=64)
-                load_words(w2_all, w2_words[0])
             for s in range(PASSES):
                 at = ((c - 1) * PASSES + s) * PACK * P
                 load_x(x_rest[:, at : at + PACK * P].rearrange("p (d t) -> p d t", d=PACK), c, s)
+        w2_all = keep.tile([P, E * N], U32, tag="words0", name="w2_all", align_bytes=64)
+        load_words(w2_all, w2_words[0])
         for q in range(QUADS):
             row = w2_from + QUAD_BLOCKS * q
             nc.sync.dma_start(
@@ -198,7 +194,10 @@ def tile_moe_wsel_b_relu2_f_kernel(
                     sums[c, r][:].rearrange("t (p u e) -> t u p e", u=2, e=2),
                     RELU,
                 )
-                h = stage.tile([P, H], BF16, tag="h", name=f"h{c}_{r}", align_bytes=64)
+                if (c, r) == (LAST, 0):
+                    h = keep.tile([P, H], BF16, tag="words0", name=f"h{c}_{r}", align_bytes=64)
+                else:
+                    h = stage.tile([P, H], BF16, tag="h", name=f"h{c}_{r}", align_bytes=64)
                 col = r * CHUNKS + c
                 nc.vector.scalar_tensor_tensor(h[:], relu[:], gate_cols[:, col : col + 1], relu[:], MULT, MULT)
                 if c < LAST:

@@ -90,11 +90,11 @@ def tile_moe_wsel_b_relu2_f_kernel(
         nc.sync.dma_start(
             out=gate_rows[gate_from:P, :], in_=gate_pieces[0 : gate_step * (GATE_ROWS - 1) + 1 : gate_step, :]
         )
-        for s in range(PASSES):
-            load_words(w1_all[s], w1_words[s])
+        load_words(w1_all[0], w1_words[0])
         for s in range(PASSES):
             x_first = keep.tile([P, PACK, P], F32, name=f"x_first{s}")
             load_x(x_first[:], 0, s)
+        load_words(w1_all[1], w1_words[1])
 
         gate_turned = psum_turn.tile([P, P], F32, tag="turn", name="gate_turned")
         nc.tensor.transpose(gate_turned[:], gate_rows[:], ident[:])
@@ -253,8 +253,8 @@ def tile_moe_wsel_b_relu2_f_kernel(
                 for a in range(OUT_TILES):
                     second_pass(accs[a][:], c, a, r)
             result = stage.tile([P, OUT_TILES, P], F32, tag="result", name=f"result{c}")
-            nc.scalar.copy(result[:, 0, :], accs[0][:])
-            nc.vector.tensor_copy(result[:, 1, :], accs[1][:])
+            nc.vector.tensor_copy(result[:, 0, :], accs[0][:])
+            nc.scalar.copy(result[:, 1, :], accs[1][:])
             nc.sync.dma_start(out=out_view[:, :, c * P : (c + 1) * P], in_=result[:])
 
         for step in range(CHUNKS + 2):

@@ -154,7 +154,7 @@ def tile_moe_wsel_b_relu2_f_kernel(
             grouped = keep.tile([P, P, PACK], BF16, name=f"x_grouped{c}_{s}", align_bytes=64)
             dst = grouped[:].rearrange("p (b e) d -> p b d e", e=4)
             src = x_raw[c, s].rearrange("p d (b e) -> p b d e", e=4)
-            if c == VECTOR_CAST_CHUNK:
+            if c >= VECTOR_CAST_CHUNK and s == PASSES - 1:
                 nc.vector.tensor_copy(dst, src)
             else:
                 nc.scalar.copy(dst, src)

@@ -52,7 +52,7 @@ def tile_moe_wsel_b_relu2_f_kernel(
         w1_rows = keep.tile([P, E * H], U8, tag="rows_then_x", name="w1_rows", align_bytes=64)
         w2_rows = keep.tile([P, E * N], U8, name="w2_rows", align_bytes=64)
         w1_all = [keep.tile([P, E * H], U32, tag=f"words{s}", name=f"w1_all{s}", align_bytes=64) for s in range(PASSES)]
-        w1_planes = keep.tile([P, G * H], U8, name="w1_planes", align_bytes=64)
+        w1_planes = keep.tile([P, PASSES * G * H], U8, name="w1_planes", align_bytes=64)
         w2_plane = keep.tile([P, G * N], U8, name="w2_plane", align_bytes=64)
         gate_rows = keep.tile([P, P], F32, name="gate_rows")
         ident = keep.tile([P, P], F32, name="ident")
@@ -78,11 +78,7 @@ def tile_moe_wsel_b_relu2_f_kernel(
             nc.sync.dma_start(out=tile[:].bitcast(I32), in_=words.rearrange("p n d -> p (n d)").bitcast(I32))
 
         nc.sync.dma_start(list1[:], offs)
-        for s in range(PASSES):
-            nc.sync.dma_start(
-                out=w1_rows[w1_from + PASS_BLOCKS * s : w1_from + PASS_BLOCKS * (s + 1), :].bitcast(I32),
-                in_=w1_scales.bitcast(I32)[s].rearrange("(q j) m -> j q m", j=QUAD_BLOCKS),
-            )
+        nc.sync.dma_start(out=w1_rows[w1_from:P, :].bitcast(I32), in_=w1_scales.bitcast(I32).rearrange("s b m -> b s m"))
         nc.sync.dma_start(list2[:], offs2)
         nc.sync.dma_start(out=w2_rows[w2_from:P, :].bitcast(I32), in_=w2_scales.bitcast(I32)[0])
         gate_pieces = gate.rearrange("r a (c t) -> (r a c) t", t=P)
@@ -107,8 +103,8 @@ def tile_moe_wsel_b_relu2_f_kernel(
         nc.vector.tensor_copy(w2_rows_sel[:], w2_rows[:].indirect(list2[:]))
         for q in range(QUADS):
             nc.sync.dma_start(
-                out=w1_planes[QUAD * q : QUAD * q + QUAD_BLOCKS * PASSES, :].bitcast(I32),
-                in_=w1_rows_sel[w1_from + q : P : QUADS, :].bitcast(I32),
+                out=w1_planes[QUAD * q : QUAD * q + QUAD_BLOCKS, :].bitcast(I32).rearrange("j (s m) -> j s m", s=PASSES),
+                in_=w1_rows_sel[w1_from + 8 * q : w1_from + 8 * (q + 1), :].bitcast(I32),
             )
 
         w1_sel_first = keep.tile([P, G * H], U32, name="w1_sel_first", align_bytes=64)
@@ -178,7 +174,7 @@ def tile_moe_wsel_b_relu2_f_kernel(
                         lhsT=x_codes[c, s][:].bitcast(FP8X4),
                         lhsT_scale=x_scales[c, s][:],
                         rhs=w1_sel[s, r].bitcast(FP8X4),
-                        rhs_scale=w1_planes[QUAD_BLOCKS * s : P, r * H : (r + 1) * H],
+                        rhs_scale=w1_planes[:, (s * G + r) * H : (s * G + r + 1) * H],
                         start=(s == 0),
                         stop=(s == PASSES - 1),
                     )

@@ -34,6 +34,7 @@ VECTOR_CAST_CHUNK = 2
 W2_GATHER_STEP = 2
 SUM_BANKS, TURN_BANKS, RESULT_BANKS = 4, 2, 2
 WARM_PASSES = 4
+W2_LOADS = 2
 
 
 def tile_moe_wsel_b_relu2_f_kernel(
@@ -127,7 +128,10 @@ def tile_moe_wsel_b_relu2_f_kernel(
                 at = ((c - 1) * PASSES + s) * PACK * P
                 load_x(x_rest[:, at : at + PACK * P].rearrange("p (d t) -> p d t", d=PACK), c, s)
         w2_all = keep.tile([P, E * N], U32, tag="words0", name="w2_all", align_bytes=64)
-        load_words(w2_all, w2_words[0])
+        w2_flat = w2_words[0].rearrange("p n d -> p (n d)").bitcast(I32)
+        for part in range(W2_LOADS):
+            cols = slice(part * E * N // W2_LOADS, (part + 1) * E * N // W2_LOADS)
+            nc.sync.dma_start(out=w2_all[:, cols].bitcast(I32), in_=w2_flat[:, cols])
         for q in range(QUADS):
             row = w2_from + QUAD_BLOCKS * q
             nc.sync.dma_start(
@@ -195,7 +199,12 @@ def tile_moe_wsel_b_relu2_f_kernel(
                 else:
                     h = stage.tile([P, H], BF16, tag="h", name=f"h{c}_{r}", align_bytes=64)
                 col = r * CHUNKS + c
-                nc.vector.scalar_tensor_tensor(h[:], relu[:], gate_cols[:, col : col + 1], relu[:], MULT, MULT)
+                parts = 2 if (c, r) == (LAST, G - 1) else 1
+                for part in range(parts):
+                    cols = slice(part * H // parts, (part + 1) * H // parts)
+                    nc.vector.scalar_tensor_tensor(
+                        h[:, cols], relu[:, cols], gate_cols[:, col : col + 1], relu[:, cols], MULT, MULT
+                    )
                 if c < LAST:
                     turned[c, r] = both[:, r : r + 1]
                 else:

@@ -34,6 +34,7 @@ VECTOR_CAST_CHUNK = 2
 W2_GATHER_STEP = 2
 SUM_BANKS, TURN_BANKS, RESULT_BANKS = 4, 2, 2
 WARM_PASSES = 4
+W1_SPLIT = 1024
 W2_LOADS = 2
 
 
@@ -88,10 +89,11 @@ def tile_moe_wsel_b_relu2_f_kernel(
             out=gate_rows[gate_from:P, :], in_=gate_pieces[0 : gate_step * (GATE_ROWS - 1) + 1 : gate_step, :]
         )
         load_words(w1_all[0], w1_words[0])
-        for s in range(PASSES):
+        last_words = w1_words[1].rearrange("p n d -> p (n d)").bitcast(I32)
+        for s, cols in enumerate((slice(0, W1_SPLIT), slice(W1_SPLIT, E * H))):
             x_first = keep.tile([P, PACK, P], F32, name=f"x_first{s}")
             load_x(x_first[:], 0, s)
-        load_words(w1_all[1], w1_words[1])
+            nc.sync.dma_start(out=w1_all[1][:, cols].bitcast(I32), in_=last_words[:, cols])
 
         gate_turned = psum_turn.tile([P, P], F32, tag="turn", name="gate_turned")
         nc.tensor.transpose(gate_turned[:], gate_rows[:], ident[:])
@@ -110,17 +112,6 @@ def tile_moe_wsel_b_relu2_f_kernel(
 
         w1_sel_first = keep.tile([P, G * H], U32, name="w1_sel_first", align_bytes=64)
         nc.vector.tensor_copy(w1_sel_first[:], w1_all[0][:].indirect(list1[:]))
-        warm = psum_result.tile([P, H], F32, tag="acc", name="warm")
-        for k in range(WARM_PASSES):
-            nc.tensor.matmul_mx(
-                out=warm[:],
-                lhsT=w1_sel_first[:, 0:P].bitcast(FP8X4),
-                lhsT_scale=w1_rows_sel[:, 0:P],
-                rhs=w1_sel_first[:, 0:H].bitcast(FP8X4),
-                rhs_scale=w1_rows_sel[:, 0:H],
-                start=True,
-                stop=True,
-            )
 
         x_rest = keep.tile([P, LAST * K], F32, tag="rows_then_x", name="x_rest", align_bytes=64)
         for c in range(1, CHUNKS):
@@ -168,6 +159,19 @@ def tile_moe_wsel_b_relu2_f_kernel(
                 scales=x_scales[c, s][:],
                 in_=x_grouped[c, s][:].rearrange("p t d -> p (t d)"),
             )
+
+        def warm_up():
+            warm = psum_result.tile([P, H], F32, tag="acc", name="warm")
+            for k in range(WARM_PASSES):
+                nc.tensor.matmul_mx(
+                    out=warm[:],
+                    lhsT=x_codes[0, 1][:].bitcast(FP8X4),
+                    lhsT_scale=x_scales[0, 1][:],
+                    rhs=w1_sel[0, 0].bitcast(FP8X4),
+                    rhs_scale=w1_rows_sel[:, 0:H],
+                    start=True,
+                    stop=True,
+                )
 
         def first_product(c):
             for r in range(G):
@@ -268,6 +272,8 @@ def tile_moe_wsel_b_relu2_f_kernel(
                     cast_x(step, s)
                 for s in range(PASSES):
                     quantize_x(step, s)
+                if step == 0:
+                    warm_up()
                 first_product(step)
             if 0 <= step - 1 < CHUNKS:
                 hidden(step - 1)

@@ -33,7 +33,6 @@ GATE_ROWS = G * CHUNKS
 VECTOR_CAST_CHUNK = 2
 W2_GATHER_STEP = 2
 SUM_BANKS, TURN_BANKS, RESULT_BANKS = 4, 2, 2
-WARM_PASSES = 4
 W1_SPLIT = 1024
 W2_LOADS = 2
 
@@ -160,19 +159,6 @@ def tile_moe_wsel_b_relu2_f_kernel(
                 in_=x_grouped[c, s][:].rearrange("p t d -> p (t d)"),
             )
 
-        def warm_up():
-            warm = psum_result.tile([P, H], F32, tag="acc", name="warm")
-            for k in range(WARM_PASSES):
-                nc.tensor.matmul_mx(
-                    out=warm[:],
-                    lhsT=x_codes[0, 1][:].bitcast(FP8X4),
-                    lhsT_scale=x_scales[0, 1][:],
-                    rhs=w1_sel[0, 0].bitcast(FP8X4),
-                    rhs_scale=w1_rows_sel[:, 0:H],
-                    start=True,
-                    stop=True,
-                )
-
         def first_product(c):
             for r in range(G):
                 sums[c, r] = psum_sum.tile([P, H], F32, tag="sum", name=f"sums{c}_{r}")
@@ -272,8 +258,6 @@ def tile_moe_wsel_b_relu2_f_kernel(
                     cast_x(step, s)
                 for s in range(PASSES):
                     quantize_x(step, s)
-                if step == 0:
-                    warm_up()
                 first_product(step)
             if 0 <= step - 1 < CHUNKS:
                 hidden(step - 1)

@@ -33,7 +33,6 @@ GATE_ROWS = G * CHUNKS
 VECTOR_CAST_CHUNK = 2
 W2_GATHER_STEP = 2
 SUM_BANKS, TURN_BANKS, RESULT_BANKS = 4, 2, 2
-W1_SPLIT = 1024
 W2_LOADS = 2
 
 
@@ -58,11 +57,12 @@ def tile_moe_wsel_b_relu2_f_kernel(
         gate_rows = keep.tile([P, P], F32, name="gate_rows")
         ident = keep.tile([P, P], F32, name="ident")
 
-        w1_from = P - PASSES * PASS_BLOCKS
-        w2_from = P - PASS_BLOCKS
+        rows_from, rows_to = QUAD, 3 * QUAD
+        w1_step = (rows_to - rows_from) // (PASSES * PASS_BLOCKS)
+        w2_step = (rows_to - rows_from) // PASS_BLOCKS
         gate_from = P - GATE_ROWS
-        nc.vector.memset(w1_rows[0:w1_from, :].bitcast(I32), 0)
-        nc.vector.memset(w2_rows[0:w2_from, :].bitcast(I32), 0)
+        nc.vector.memset(w1_rows[:].bitcast(I32), 0)
+        nc.vector.memset(w2_rows[:].bitcast(I32), 0)
         nc.gpsimd.memset(gate_rows[0:gate_from, :], 0.0)
         make_identity(nc, ident[:])
         nc.gpsimd.memset(w1_planes[:].bitcast(I32), 0)
@@ -79,20 +79,21 @@ def tile_moe_wsel_b_relu2_f_kernel(
             nc.sync.dma_start(out=tile[:].bitcast(I32), in_=words.rearrange("p n d -> p (n d)").bitcast(I32))
 
         nc.sync.dma_start(list1[:], offs)
-        nc.sync.dma_start(out=w1_rows[w1_from:P, :].bitcast(I32), in_=w1_scales.bitcast(I32).rearrange("s b m -> b s m"))
-        nc.sync.dma_start(list2[:], offs2)
-        nc.sync.dma_start(out=w2_rows[w2_from:P, :].bitcast(I32), in_=w2_scales.bitcast(I32)[0])
+        nc.scalar.dma_start(
+            out=w1_rows[rows_from:rows_to:w1_step, :].bitcast(I32), in_=w1_scales.bitcast(I32).rearrange("s b m -> b s m")
+        )
+        nc.scalar.dma_start(out=w2_rows[rows_from:rows_to:w2_step, :].bitcast(I32), in_=w2_scales.bitcast(I32)[0])
         gate_pieces = gate.rearrange("r a (c t) -> (r a c) t", t=P)
         gate_step = P + 1
-        nc.sync.dma_start(
+        nc.scalar.dma_start(
             out=gate_rows[gate_from:P, :], in_=gate_pieces[0 : gate_step * (GATE_ROWS - 1) + 1 : gate_step, :]
         )
         load_words(w1_all[0], w1_words[0])
-        last_words = w1_words[1].rearrange("p n d -> p (n d)").bitcast(I32)
-        for s, cols in enumerate((slice(0, W1_SPLIT), slice(W1_SPLIT, E * H))):
+        nc.sync.dma_start(list2[:], offs2)
+        for s in range(PASSES):
             x_first = keep.tile([P, PACK, P], F32, name=f"x_first{s}")
             load_x(x_first[:], 0, s)
-            nc.sync.dma_start(out=w1_all[1][:, cols].bitcast(I32), in_=last_words[:, cols])
+        load_words(w1_all[1], w1_words[1])
 
         gate_turned = psum_turn.tile([P, P], F32, tag="turn", name="gate_turned")
         nc.tensor.transpose(gate_turned[:], gate_rows[:], ident[:])
@@ -106,7 +107,7 @@ def tile_moe_wsel_b_relu2_f_kernel(
         for q in range(QUADS):
             nc.sync.dma_start(
                 out=w1_planes[QUAD * q : QUAD * q + QUAD_BLOCKS, :].bitcast(I32).rearrange("j (s m) -> j s m", s=PASSES),
-                in_=w1_rows_sel[w1_from + 8 * q : w1_from + 8 * (q + 1), :].bitcast(I32),
+                in_=w1_rows_sel[rows_from + 16 * q : rows_from + 16 * (q + 1) : w1_step, :].bitcast(I32),
             )
 
         w1_sel_first = keep.tile([P, G * H], U32, name="w1_sel_first", align_bytes=64)
@@ -123,10 +124,10 @@ def tile_moe_wsel_b_relu2_f_kernel(
             cols = slice(part * E * N // W2_LOADS, (part + 1) * E * N // W2_LOADS)
             nc.sync.dma_start(out=w2_all[:, cols].bitcast(I32), in_=w2_flat[:, cols])
         for q in range(QUADS):
-            row = w2_from + QUAD_BLOCKS * q
+            row = rows_from + 16 * q
             nc.sync.dma_start(
                 out=w2_plane[QUAD * q : QUAD * q + QUAD_BLOCKS, :].bitcast(I32),
-                in_=w2_rows_sel[row : row + QUAD_BLOCKS, :].bitcast(I32),
+                in_=w2_rows_sel[row : row + 16 : w2_step, :].bitcast(I32),
             )
 
         w1_sel = {}

@@ -57,12 +57,13 @@ def tile_moe_wsel_b_relu2_f_kernel(
         gate_rows = keep.tile([P, P], F32, name="gate_rows")
         ident = keep.tile([P, P], F32, name="ident")
 
-        rows_from, rows_to = QUAD, 3 * QUAD
-        w1_step = (rows_to - rows_from) // (PASSES * PASS_BLOCKS)
-        w2_step = (rows_to - rows_from) // PASS_BLOCKS
+        w1_from = P - PASSES * PASS_BLOCKS
+        w2_to = P // 2
+        w2_from = w2_to - PASS_BLOCKS
         gate_from = P - GATE_ROWS
-        nc.vector.memset(w1_rows[:].bitcast(I32), 0)
-        nc.vector.memset(w2_rows[:].bitcast(I32), 0)
+        nc.vector.memset(w1_rows[0:w1_from, :].bitcast(I32), 0)
+        nc.vector.memset(w2_rows[0:w2_from, :].bitcast(I32), 0)
+        nc.vector.memset(w2_rows[w2_to:P, :].bitcast(I32), 0)
         nc.gpsimd.memset(gate_rows[0:gate_from, :], 0.0)
         make_identity(nc, ident[:])
         nc.gpsimd.memset(w1_planes[:].bitcast(I32), 0)
@@ -80,9 +81,9 @@ def tile_moe_wsel_b_relu2_f_kernel(
 
         nc.sync.dma_start(list1[:], offs)
         nc.scalar.dma_start(
-            out=w1_rows[rows_from:rows_to:w1_step, :].bitcast(I32), in_=w1_scales.bitcast(I32).rearrange("s b m -> b s m")
+            out=w1_rows[w1_from:P, :].bitcast(I32), in_=w1_scales.bitcast(I32).rearrange("s b m -> b s m")
         )
-        nc.scalar.dma_start(out=w2_rows[rows_from:rows_to:w2_step, :].bitcast(I32), in_=w2_scales.bitcast(I32)[0])
+        nc.scalar.dma_start(out=w2_rows[w2_from:w2_to, :].bitcast(I32), in_=w2_scales.bitcast(I32)[0])
         gate_pieces = gate.rearrange("r a (c t) -> (r a c) t", t=P)
         gate_step = P + 1
         nc.scalar.dma_start(
@@ -107,7 +108,7 @@ def tile_moe_wsel_b_relu2_f_kernel(
         for q in range(QUADS):
             nc.sync.dma_start(
                 out=w1_planes[QUAD * q : QUAD * q + QUAD_BLOCKS, :].bitcast(I32).rearrange("j (s m) -> j s m", s=PASSES),
-                in_=w1_rows_sel[rows_from + 16 * q : rows_from + 16 * (q + 1) : w1_step, :].bitcast(I32),
+                in_=w1_rows_sel[w1_from + 8 * q : w1_from + 8 * (q + 1), :].bitcast(I32),
             )
 
         w1_sel_first = keep.tile([P, G * H], U32, name="w1_sel_first", align_bytes=64)
@@ -124,10 +125,10 @@ def tile_moe_wsel_b_relu2_f_kernel(
             cols = slice(part * E * N // W2_LOADS, (part + 1) * E * N // W2_LOADS)
             nc.sync.dma_start(out=w2_all[:, cols].bitcast(I32), in_=w2_flat[:, cols])
         for q in range(QUADS):
-            row = rows_from + 16 * q
+            row = w2_from + QUAD_BLOCKS * q
             nc.sync.dma_start(
                 out=w2_plane[QUAD * q : QUAD * q + QUAD_BLOCKS, :].bitcast(I32),
-                in_=w2_rows_sel[row : row + 16 : w2_step, :].bitcast(I32),
+                in_=w2_rows_sel[row : row + QUAD_BLOCKS, :].bitcast(I32),
             )
 
         w1_sel = {}

@@ -73,7 +73,8 @@ def tile_moe_wsel_b_relu2_f_kernel(
 
         def load_x(piece, c, s):
             rows = xT[s * P * PACK : (s + 1) * P * PACK, c * P : (c + 1) * P]
-            nc.sync.dma_start(out=piece, in_=rows.rearrange("(p d) t -> p d t", d=PACK))
+            queue = nc.scalar if c == 0 else nc.sync
+            queue.dma_start(out=piece, in_=rows.rearrange("(p d) t -> p d t", d=PACK))
             x_raw[c, s] = piece
 
         def load_words(tile, words):
@@ -86,11 +87,11 @@ def tile_moe_wsel_b_relu2_f_kernel(
         nc.scalar.dma_start(out=w2_rows[w2_from:w2_to, :].bitcast(I32), in_=w2_scales.bitcast(I32)[0])
         gate_pieces = gate.rearrange("r a (c t) -> (r a c) t", t=P)
         gate_step = P + 1
-        nc.scalar.dma_start(
+        nc.sync.dma_start(list2[:], offs2)
+        load_words(w1_all[0], w1_words[0])
+        nc.sync.dma_start(
             out=gate_rows[gate_from:P, :], in_=gate_pieces[0 : gate_step * (GATE_ROWS - 1) + 1 : gate_step, :]
         )
-        load_words(w1_all[0], w1_words[0])
-        nc.sync.dma_start(list2[:], offs2)
         for s in range(PASSES):
             x_first = keep.tile([P, PACK, P], F32, name=f"x_first{s}")
             load_x(x_first[:], 0, s)

@@ -27,6 +27,7 @@ QUAD = 32
 QUADS = P // QUAD
 QUAD_BLOCKS = 4
 PASS_BLOCKS = QUADS * QUAD_BLOCKS
+MOVE_ORDER = (0, 2, 1, 3)
 LIST_GROUP = 16
 GATE_ROWS = G * CHUNKS
 
@@ -106,7 +107,7 @@ def tile_moe_wsel_b_relu2_f_kernel(
         nc.vector.tensor_copy(w1_rows_sel[:], w1_rows[:].indirect(list1[:]))
         w2_rows_sel = keep.tile([P, G * N], U8, name="w2_rows_sel", align_bytes=64)
         nc.vector.tensor_copy(w2_rows_sel[:], w2_rows[:].indirect(list2[:]))
-        for q in range(QUADS):
+        for q in MOVE_ORDER:
             nc.sync.dma_start(
                 out=w1_planes[QUAD * q : QUAD * q + QUAD_BLOCKS, :].bitcast(I32).rearrange("j (s m) -> j s m", s=PASSES),
                 in_=w1_rows_sel[w1_from + 8 * q : w1_from + 8 * (q + 1), :].bitcast(I32),
@@ -125,7 +126,7 @@ def tile_moe_wsel_b_relu2_f_kernel(
         for part in range(W2_LOADS):
             cols = slice(part * E * N // W2_LOADS, (part + 1) * E * N // W2_LOADS)
             nc.sync.dma_start(out=w2_all[:, cols].bitcast(I32), in_=w2_flat[:, cols])
-        for q in range(QUADS):
+        for q in MOVE_ORDER:
             row = w2_from + QUAD_BLOCKS * q
             nc.sync.dma_start(
                 out=w2_plane[QUAD * q : QUAD * q + QUAD_BLOCKS, :].bitcast(I32),

from contextlib import ExitStack

import concourse.mybir as mybir
from concourse.masks import make_identity

K, T, E, G, H, N = 1024, 512, 6, 2, 512, 256
FLOPS = 2 * G * T * H * (K + N)

F32 = mybir.dt.float32
BF16 = mybir.dt.bfloat16
I32 = mybir.dt.int32
U32 = mybir.dt.uint32
U16 = mybir.dt.uint16
U8 = mybir.dt.uint8
FP8X4 = mybir.dt.float8_e4m3fn_x4
MULT = mybir.AluOpType.mult
RELU = mybir.ActivationFunctionType.Relu
COPY = mybir.ActivationFunctionType.Copy

P = 128
PACK = 4
PASSES = K // (P * PACK)
CHUNKS = T // P
LAST = CHUNKS - 1
OUT_TILES = N // P
QUAD = 32
QUADS = P // QUAD
QUAD_BLOCKS = 4
PASS_BLOCKS = QUADS * QUAD_BLOCKS
MOVE_ORDER = (0, 2, 1, 3)
LIST_GROUP = 16
GATE_ROWS = G * CHUNKS

VECTOR_CAST_CHUNK = 2
W2_GATHER_STEP = 2
SUM_BANKS, TURN_BANKS, RESULT_BANKS = 4, 2, 2
W2_LOADS = 2


def tile_moe_wsel_b_relu2_f_kernel(
    tc, xT, w1_words, w1_scales, w2_words, w2_scales, gate, offs, offs2, out
):
    nc = tc.nc
    with ExitStack() as ctx:
        keep = ctx.enter_context(tc.tile_pool(name="keep", bufs=1))
        stage = ctx.enter_context(tc.tile_pool(name="stage", bufs=G * CHUNKS))
        psum_sum = ctx.enter_context(tc.psum_pool(name="psum_sum", bufs=SUM_BANKS))
        psum_turn = ctx.enter_context(tc.psum_pool(name="psum_turn", bufs=TURN_BANKS))
        psum_result = ctx.enter_context(tc.psum_pool(name="psum_result", bufs=RESULT_BANKS))

        list1 = keep.tile([P, G * H // LIST_GROUP], U16, name="list1")
        list2 = keep.tile([P, G * N // LIST_GROUP], U16, name="list2")
        w1_rows = keep.tile([P, E * H], U8, tag="rows_then_x", name="w1_rows", align_bytes=64)
        w2_rows = keep.tile([P, E * N], U8, name="w2_rows", align_bytes=64)
        w1_all = [keep.tile([P, E * H], U32, tag=f"words{s}", name=f"w1_all{s}", align_bytes=64) for s in range(PASSES)]
        w1_planes = keep.tile([P, PASSES * G * H], U8, name="w1_planes", align_bytes=64)
        w2_plane = keep.tile([P, G * N], U8, name="w2_plane", align_bytes=64)
        gate_rows = keep.tile([P, P], F32, name="gate_rows")
        ident = keep.tile([P, P], F32, name="ident")

        w1_from = P - PASSES * PASS_BLOCKS
        w2_to = P // 2
        w2_from = w2_to - PASS_BLOCKS
        gate_from = P - GATE_ROWS
        nc.vector.memset(w1_rows[0:w1_from, :].bitcast(I32), 0)
        nc.vector.memset(w2_rows[0:w2_from, :].bitcast(I32), 0)
        nc.vector.memset(w2_rows[w2_to:P, :].bitcast(I32), 0)
        nc.gpsimd.memset(gate_rows[0:gate_from, :], 0.0)
        make_identity(nc, ident[:])
        nc.gpsimd.memset(w1_planes[:].bitcast(I32), 0)
        nc.gpsimd.memset(w2_plane[:].bitcast(I32), 0)

        x_raw = {}

        def load_x(piece, c, s):
            rows = xT[s * P * PACK : (s + 1) * P * PACK, c * P : (c + 1) * P]
            queue = nc.scalar if c == 0 else nc.sync
            queue.dma_start(out=piece, in_=rows.rearrange("(p d) t -> p d t", d=PACK))
            x_raw[c, s] = piece

        def load_words(tile, words):
            nc.sync.dma_start(out=tile[:].bitcast(I32), in_=words.rearrange("p n d -> p (n d)").bitcast(I32))

        nc.sync.dma_start(list1[:], offs)
        nc.scalar.dma_start(
            out=w1_rows[w1_from:P, :].bitcast(I32), in_=w1_scales.bitcast(I32).rearrange("s b m -> b s m")
        )
        nc.scalar.dma_start(out=w2_rows[w2_from:w2_to, :].bitcast(I32), in_=w2_scales.bitcast(I32)[0])
        gate_pieces = gate.rearrange("r a (c t) -> (r a c) t", t=P)
        gate_step = P + 1
        nc.sync.dma_start(list2[:], offs2)
        load_words(w1_all[0], w1_words[0])
        nc.sync.dma_start(
            out=gate_rows[gate_from:P, :], in_=gate_pieces[0 : gate_step * (GATE_ROWS - 1) + 1 : gate_step, :]
        )
        for s in range(PASSES):
            x_first = keep.tile([P, PACK, P], F32, name=f"x_first{s}")
            load_x(x_first[:], 0, s)
        load_words(w1_all[1], w1_words[1])

        gate_turned = psum_turn.tile([P, P], F32, tag="turn", name="gate_turned")
        nc.tensor.transpose(gate_turned[:], gate_rows[:], ident[:])
        gate_cols = keep.tile([P, GATE_ROWS], F32, name="gate_cols")
        nc.scalar.activation(gate_cols[:], gate_turned[:, gate_from:P], COPY)

        w1_rows_sel = keep.tile([P, G * H], U8, name="w1_rows_sel", align_bytes=64)
        nc.vector.tensor_copy(w1_rows_sel[:], w1_rows[:].indirect(list1[:]))
        w2_rows_sel = keep.tile([P, G * N], U8, name="w2_rows_sel", align_bytes=64)
        nc.vector.tensor_copy(w2_rows_sel[:], w2_rows[:].indirect(list2[:]))
        for q in MOVE_ORDER:
            nc.sync.dma_start(
                out=w1_planes[QUAD * q : QUAD * q + QUAD_BLOCKS, :].bitcast(I32).rearrange("j (s m) -> j s m", s=PASSES),
                in_=w1_rows_sel[w1_from + 8 * q : w1_from + 8 * (q + 1), :].bitcast(I32),
            )

        w1_sel_first = keep.tile([P, G * H], U32, name="w1_sel_first", align_bytes=64)
        nc.vector.tensor_copy(w1_sel_first[:], w1_all[0][:].indirect(list1[:]))

        x_rest = keep.tile([P, LAST * K], F32, tag="rows_then_x", name="x_rest", align_bytes=64)
        for c in range(1, CHUNKS):
            for s in range(PASSES):
                at = ((c - 1) * PASSES + s) * PACK * P
                load_x(x_rest[:, at : at + PACK * P].rearrange("p (d t) -> p d t", d=PACK), c, s)
        w2_all = keep.tile([P, E * N], U32, tag="words0", name="w2_all", align_bytes=64)
        w2_flat = w2_words[0].rearrange("p n d -> p (n d)").bitcast(I32)
        for part in range(W2_LOADS):
            cols = slice(part * E * N // W2_LOADS, (part + 1) * E * N // W2_LOADS)
            nc.sync.dma_start(out=w2_all[:, cols].bitcast(I32), in_=w2_flat[:, cols])
        for q in MOVE_ORDER:
            row = w2_from + QUAD_BLOCKS * q
            nc.sync.dma_start(
                out=w2_plane[QUAD * q : QUAD * q + QUAD_BLOCKS, :].bitcast(I32),
                in_=w2_rows_sel[row : row + QUAD_BLOCKS, :].bitcast(I32),
            )

        w1_sel = {}
        for r in range(G):
            w1_sel[0, r] = w1_sel_first[:, r * H : (r + 1) * H]
            second = keep.tile([P, H], U32, name=f"w1_sel_second{r}", align_bytes=64)
            entries = list1[:, r * H // LIST_GROUP : (r + 1) * H // LIST_GROUP]
            nc.vector.tensor_copy(second[:], w1_all[1][:].indirect(entries))
            w1_sel[1, r] = second[:]
        w2_sel = keep.tile([P, G * N], U32, name="w2_sel", align_bytes=64)

        x_grouped, x_codes, x_scales, sums, turned, h_codes, h_scales = {}, {}, {}, {}, {}, {}, {}

        def cast_x(c, s):
            grouped = keep.tile([P, P, PACK], BF16, name=f"x_grouped{c}_{s}", align_bytes=64)
            dst = grouped[:].rearrange("p (b e) d -> p b d e", e=4)
            src = x_raw[c, s].rearrange("p d (b e) -> p b d e", e=4)
            if c >= VECTOR_CAST_CHUNK and s == PASSES - 1:
                nc.vector.tensor_copy(dst, src)
            else:
                nc.scalar.copy(dst, src)
            x_grouped[c, s] = grouped

        def quantize_x(c, s):
            x_codes[c, s] = keep.tile([P, P], U32, name=f"x_codes{c}_{s}", align_bytes=64)
            x_scales[c, s] = keep.tile([P, P], U8, name=f"x_scales{c}_{s}", align_bytes=64)
            nc.vector.quantize_mx(
                out=x_codes[c, s][:].bitcast(FP8X4),
                scales=x_scales[c, s][:],
                in_=x_grouped[c, s][:].rearrange("p t d -> p (t d)"),
            )

        def first_product(c):
            for r in range(G):
                sums[c, r] = psum_sum.tile([P, H], F32, tag="sum", name=f"sums{c}_{r}")
                for s in range(PASSES):
                    nc.tensor.matmul_mx(
                        out=sums[c, r][:],
                        lhsT=x_codes[c, s][:].bitcast(FP8X4),
                        lhsT_scale=x_scales[c, s][:],
                        rhs=w1_sel[s, r].bitcast(FP8X4),
                        rhs_scale=w1_planes[:, (s * G + r) * H : (s * G + r + 1) * H],
                        start=(s == 0),
                        stop=(s == PASSES - 1),
                    )

        def hidden(c):
            if c < LAST:
                both = psum_turn.tile([P, G, 2, P], F32, tag="turn", name=f"turned{c}")
                turned[c] = both[:]
            for r in range(G):
                relu = stage.tile([P, H], F32, tag="relu", name=f"relu{c}_{r}")
                nc.scalar.activation(
                    relu[:].rearrange("t (u p e) -> t u p e", u=2, e=2),
                    sums[c, r][:].rearrange("t (p u e) -> t u p e", u=2, e=2),
                    RELU,
                )
                if (c, r) == (LAST, 0):
                    h = keep.tile([P, H], BF16, tag="words0", name=f"h{c}_{r}", align_bytes=64)
                else:
                    h = stage.tile([P, H], BF16, tag="h", name=f"h{c}_{r}", align_bytes=64)
                col = r * CHUNKS + c
                parts = 2 if (c, r) == (LAST, G - 1) else 1
                for part in range(parts):
                    cols = slice(part * H // parts, (part + 1) * H // parts)
                    nc.vector.scalar_tensor_tensor(
                        h[:, cols], relu[:, cols], gate_cols[:, col : col + 1], relu[:, cols], MULT, MULT
                    )
                if c < LAST:
                    turned[c, r] = both[:, r : r + 1]
                else:
                    alone = psum_sum.tile([P, 1, 2, P], F32, tag="sum", name=f"turned{c}_{r}")
                    turned[c, r] = alone[:]
                pairs = h[:].bitcast(F32)
                for u in range(2):
                    nc.tensor.transpose(turned[c, r][:, 0, u, :], pairs[:, u * P : (u + 1) * P], ident[:])

        def quantize_h(c, source, experts):
            width = len(experts) * P
            label = f"{c}_{experts[0]}"
            grouped = stage.tile([P, width * PACK], BF16, tag="h_grouped", name="h_grouped" + label, align_bytes=64)
            nc.scalar.copy(
                grouped[:].bitcast(F32).rearrange("p (r t u) -> p r t u", t=P, u=2),
                source.rearrange("p r u t -> p r t u"),
            )
            codes = keep.tile([P, width], U32, name="h_codes" + label, align_bytes=64)
            scales = keep.tile([P, width], U8, name="h_scales" + label, align_bytes=64)
            nc.vector.quantize_mx(out=codes[:].bitcast(FP8X4), scales=scales[:], in_=grouped[:])
            for place, r in enumerate(experts):
                h_codes[c, r] = codes[:, place * P : (place + 1) * P]
                h_scales[c, r] = scales[:, place * P : (place + 1) * P]

        def second_pass(target, c, a, r):
            cols = slice(r * N + a * P, r * N + (a + 1) * P)
            nc.tensor.matmul_mx(
                out=target,
                lhsT=w2_sel[:, cols].bitcast(FP8X4),
                lhsT_scale=w2_plane[:, cols],
                rhs=h_codes[c, r].bitcast(FP8X4),
                rhs_scale=h_scales[c, r],
                start=(r == 0),
                stop=(r == G - 1),
            )

        out_view = out.rearrange("(a p) t -> p a t", p=P)

        def second_product(c):
            acc = psum_result.tile([P, OUT_TILES, P], F32, tag="acc", name=f"acc{c}")
            for a in range(OUT_TILES):
                for r in range(G):
                    second_pass(acc[:, a, :], c, a, r)
            result = stage.tile([P, OUT_TILES, P], F32, tag="result", name=f"result{c}")
            nc.scalar.copy(result[:], acc[:])
            nc.sync.dma_start(out=out_view[:, :, c * P : (c + 1) * P], in_=result[:])

        def last_second_product(c):
            accs = [psum_sum.tile([P, P], F32, tag="sum", name=f"last_acc{a}") for a in range(OUT_TILES)]
            for r in range(G):
                for a in range(OUT_TILES):
                    second_pass(accs[a][:], c, a, r)
            result = stage.tile([P, OUT_TILES, P], F32, tag="result", name=f"result{c}")
            nc.vector.tensor_copy(result[:, 0, :], accs[0][:])
            nc.scalar.copy(result[:, 1, :], accs[1][:])
            nc.sync.dma_start(out=out_view[:, :, c * P : (c + 1) * P], in_=result[:])

        for step in range(CHUNKS + 2):
            if step < CHUNKS:
                for s in range(PASSES):
                    cast_x(step, s)
                for s in range(PASSES):
                    quantize_x(step, s)
                first_product(step)
            if 0 <= step - 1 < CHUNKS:
                hidden(step - 1)
            if step == W2_GATHER_STEP:
                nc.vector.tensor_copy(w2_sel[:], w2_all[:].indirect(list2[:]))
            if 0 <= step - 2 < LAST:
                quantize_h(step - 2, turned[step - 2], tuple(range(G)))
                second_product(step - 2)
            if step - 2 == LAST:
                for r in range(G):
                    quantize_h(LAST, turned[LAST, r], (r,))
                last_second_product(LAST)
